import numpy as np, ml_dtypes
CORES = [24,26,29,31,48,50,53,55]
N = 8
GR, GC = 2, 4
L, KA, KB, F = 4, 1, 2, 128
def setup_inputs(rng):
    return {"a": rng.standard_normal((N, 128, KA * 128), dtype=np.float32).astype(ml_dtypes.bfloat16), "b": rng.standard_normal((N, 128, KB * F), dtype=np.float32).astype(ml_dtypes.bfloat16)}
def setup_inputs_big(rng):
    d = setup_inputs(rng)
    for k in ("a", "b"): d[k] = (d[k].astype(np.float32) * 1024.0).astype(d[k].dtype)
    return d
def setup_inputs_small(rng):
    d = setup_inputs(rng)
    for k in ("a", "b"): d[k] = (d[k].astype(np.float32) * (1 / 1024.0)).astype(d[k].dtype)
    return d
def setup_inputs_apart(rng):
    d = setup_inputs(rng)
    f = (10.0 ** rng.permutation(np.linspace(-1.5, 1.5, N))).astype(np.float32).reshape(N, 1, 1)
    for k in ("a", "b"): d[k] = (d[k].astype(np.float32) * f).astype(d[k].dtype)
    return d
def reference(a, b):
    A, B = a.astype(np.float64), b.astype(np.float64)
    y = np.zeros((N, 128, F))
    for i in range(GR):
        for j in range(GC):
            for k in range(L):
                At = A[i * GC + k // KA][:, 128 * (k % KA):128 * (k % KA) + 128]
                Bt = B[(k // KB) * GC + j][:, F * (k % KB):F * (k % KB) + F]
                y[i * GC + j] += At.T @ Bt
    return {"y": y.astype(ml_dtypes.bfloat16 if a.dtype != np.float64 else np.float64)}

from concourse.bass import DstId, RemoteDMATransfer

GR, GC = 2, 4
KB, F = 2, 128
P = 128

SCRATCH = {
    "ag": ("sbuf", [P, GC * P], "bfloat16"),
    "bg": ("sbuf", [P, GR * KB * F], "bfloat16"),
    "bd": ("dram", [P, KB * F], "bfloat16"),
    "rl": ("dram", [P, KB * F], "bfloat16"),
    "ps": ("psum", [P, F], "float32"),
    "ys": ("sbuf", [P, F], "bfloat16"),
}
SEMAPHORES = ["lda", "ldb", "ldr", "arra", "arrb", "rel", "sent", "mm", "cp", "st"]

N_X = 8
N_A = 8
N_R = 8


def _pick(mask, n, avoid=0):
    bits = [e for e in range(mask.bit_length()) if (mask >> e) & 1]
    bits = [e for e in bits if not (avoid >> e) & 1] + [e for e in bits if (avoid >> e) & 1]
    out = 0
    for e in bits[:n]:
        out |= 1 << e
    return out


def rank_program(g, core, T, topo):
    rank = T.rank_of(core)
    if rank is None:
        return
    S = T.sem
    i, j = divmod(rank, GC)
    row = [T.cores[i * GC + k] for k in range(GC)]
    mates_on_chip = [c for c in row if c != core]

    def partner(c):
        r = T.rank_of(c)
        return T.cores[(GR - 1 - r // GC) * GC + r % GC]

    def relay_of(c):
        if topo.may_write(c, partner(c)):
            return None
        can = [r for r in row if r != c and topo.may_write(r, partner(c)) and topo.may_write(c, r)]
        same = [r for r in can if topo.die(r) == topo.die(c)]
        return (same or can)[0]

    own_a = T.ag[:, P * j:P * (j + 1)]
    own_b = T.bg[:, KB * F * i:KB * F * (i + 1)]
    relay = relay_of(core)
    clients = [c for c in mates_on_chip if relay_of(c) == core]

    on_mask = topo.mask(core, mates_on_chip[0])
    for c in mates_on_chip:
        on_mask &= topo.mask(core, c)
    off_mask = topo.mask(core, partner(core))
    m_x = _pick(off_mask, N_X)
    m_a = _pick(on_mask, N_A, avoid=off_mask)
    m_r = _pick(on_mask, N_R)

    if relay is None:
        g.sync.dma_start(own_b, T.b[:]).then_inc(S.ldb, 16)
        g.scalar.dma_start(own_a, T.a[:]).then_inc(S.lda, 16)
    else:
        g.sync.dma_start(T.bd[:], T.b[:]).then_inc(S.ldr, 16)
        g.scalar.dma_start(own_a, T.a[:]).then_inc(S.lda, 16)
        g.sync.dma_start(own_b, T.b[:]).then_inc(S.ldb, 16)

    sent = 0
    if relay is None:
        rid, pid, _ = topo.addr(partner(core))
        g.wait_ge(S.ldb, 16)
        g.remote_dma(out_ap=own_b, in_ap=own_b, remote_sem=S.arrb, local_sem=S.sent,
                     pid=pid, routing_id=rid, dma_engine_mask=m_x)
        sent += N_X
    else:
        rid, pid, _ = topo.addr(relay)
        g.wait_ge(S.ldr, 16)
        g.remote_dma(out_ap=T.rl[:], in_ap=T.bd[:], remote_sem=S.rel, local_sem=S.sent,
                     pid=pid, routing_id=rid, dma_engine_mask=m_r)
        sent += N_R

    g.wait_ge(S.lda, 16)
    ids = [DstId(rid=topo.addr(c)[0], pnc=topo.addr(c)[1]) for c in mates_on_chip]
    g.remote_dma_fused([RemoteDMATransfer(dst_ids=ids, dma_engine_mask=m_a, remote_sem=S.arra,
                                          srcs=[own_a], dsts=[own_a for _ in mates_on_chip])],
                       local_sem=S.sent)
    sent += N_A

    for c in clients:
        rid, pid, _ = topo.addr(partner(c))
        g.wait_ge(S.rel, N_R)
        g.remote_dma(out_ap=own_b, in_ap=T.rl[:], remote_sem=S.arrb, local_sem=S.sent,
                     pid=pid, routing_id=rid, dma_engine_mask=m_x)
        sent += N_X
    g.wait_ge(S.sent, sent)

    mine = [KB * i + t for t in range(KB)]
    theirs = [k for k in range(GR * KB) if k not in mine]
    te = g.tensor
    te.wait_ge(S.lda, 16)
    te.wait_ge(S.ldb, 16)
    te.wait_ge(S.arra, N_A * len(mates_on_chip))
    order = mine + theirs
    for n, k in enumerate(order):
        if k == theirs[0]:
            te.wait_ge(S.arrb, N_X)
        mm = te.matmul(T.ps[:], T.ag[:, P * k:P * (k + 1)], T.bg[:, F * k:F * (k + 1)],
                       start=(n == 0), stop=(n == len(order) - 1))
    mm.then_inc(S.mm, 1)

    g.vector.wait_ge(S.mm, 1)
    g.vector.tensor_copy(T.ys[:], T.ps[:]).then_inc(S.cp, 1)

    g.sync.wait_ge(S.cp, 1)
    g.sync.dma_start(T.y[:], T.ys[:]).then_inc(S.st, 16)
    g.sync.wait_ge(S.st, 16)
